import numpy as np
import ml_dtypes


def mxq(x, axis, fmt="e4m3"):
    dtype, down = {"e4m3": (ml_dtypes.float8_e4m3fn, 7), "e5m2": (ml_dtypes.float8_e5m2, 14)}[fmt]
    v = np.moveaxis(np.asarray(x, np.float32).astype(ml_dtypes.bfloat16).astype(np.float64), axis, -1)
    blocks = v.reshape(v.shape[:-1] + (-1, 32))
    amax = np.abs(blocks).max(-1, keepdims=True)
    byte = np.maximum(np.where(amax > 0, np.frexp(amax)[1] - 1 + 127, 0) - down, 1)
    scale = np.exp2(byte - 127.0)
    codes = (blocks / scale).astype(np.float32).astype(dtype).astype(np.float64)
    return np.moveaxis((codes * scale).reshape(v.shape), -1, axis)


WIDE = False


def mx_kscale(k):
    if not WIDE:
        return np.ones(k)
    levels = np.array([10, -10, 5, -5, 0])
    if k % 512:
        return np.exp2(np.random.permutation(np.resize(levels, k // 32))).repeat(32)
    a = np.empty((k // 512, 16))
    for p in range(k // 512):
        a[p, :8] = np.random.permutation(np.resize(levels, 8))
        for g in range(8):
            far = levels[np.abs(levels - a[p, g]) >= 10]
            a[p, g + 8] = far[np.random.randint(len(far))]
    return np.exp2(a.ravel()).repeat(32)


def f64(x):
    return np.asarray(x).astype(np.float64)


def striped(idx):
    return np.tile(idx.reshape(-1, 16).T, (8, 1)).astype(np.uint16)


def unstriped(offs):
    return offs[:16].T.reshape(-1).astype(np.int64)


E2M1 = np.array([0.0, 0.5, 1.0, 1.5, 2.0, 3.0, 4.0, 6.0, -0.0, -0.5, -1.0, -1.5, -2.0, -3.0, -4.0, -6.0])


def pack_weight(w, fmt):
    k, n = w.shape
    w = f64(np.asarray(w, np.float32).astype(ml_dtypes.bfloat16)).reshape(k // 32, 32, n)
    amax = np.abs(w).max(1)
    if fmt == "e4m3":
        byte = np.frexp(amax)[1] - 1 + 127 - 7
    else:
        mant, ex = np.frexp(amax / 6.0)
        byte = np.where(mant > 0.5, ex, ex - 1) + 127
    byte = np.clip(np.where(amax > 0, byte, 1), 1, 254)
    scaled = (w * np.exp2(127.0 - byte)[:, None, :]).reshape(k, n).astype(np.float32)
    by_word = np.ascontiguousarray(scaled.reshape(k // 512, 128, 4, n).transpose(0, 1, 3, 2))
    if fmt == "e4m3":
        words = by_word.astype(ml_dtypes.float8_e4m3fn).view(np.uint8)
    else:
        c = by_word.astype(ml_dtypes.float4_e2m1fn).view(np.uint8) & 0xF
        words = (c[..., 0::2] | (c[..., 1::2] << 4)).reshape(k // 512, 128, 2 * n)
    return np.ascontiguousarray(words), np.ascontiguousarray(byte.astype(np.uint8).reshape(k // 512, 16, n))


def unpack_weight(words, scales, fmt):
    g, _, n = scales.shape
    words = np.ascontiguousarray(words).reshape(g, 128, n, -1)
    if fmt == "e4m3":
        vals = words.view(ml_dtypes.float8_e4m3fn).astype(np.float64)
    else:
        nib = np.empty((g, 128, n, 4), np.uint8)
        nib[..., 0::2] = words & 0xF
        nib[..., 1::2] = words >> 4
        vals = E2M1[nib]
    vals = vals * np.repeat(np.exp2(scales.astype(np.float64) - 127.0), 8, axis=1)[..., None]
    return vals.transpose(0, 1, 3, 2).reshape(g * 512, n)


def gelu(v):
    return 0.5 * v * (1.0 + np.tanh(np.sqrt(2.0 / np.pi) * (v + 0.044715 * v**3)))


K, H, T, S, T2, T3, S2, P = 512, 1024, 2048, 1024, 2048, 2048, 512, 1024

def setup_inputs():
    n = np.random.standard_normal
    s = mx_kscale(K)[:, None]
    u = mx_kscale(H)[:, None]
    tab_words, tab_scales = pack_weight(n((K, T)) * s, "e4m3")
    tab2_words, tab2_scales = pack_weight(n((H, T3)) / np.sqrt(H) / u, "e4m3")
    wg_words, wg_scales = pack_weight(1.5 * n((K, H)) / np.sqrt(K) / s, "e2m1")
    return {
        "tab_words": tab_words, "tab_scales": tab_scales,
        "tab2_words": tab2_words, "tab2_scales": tab2_scales,
        "wg_words": wg_words, "wg_scales": wg_scales,
        "wb": (n((K, H)) / np.sqrt(K) / s * u.T).astype(np.float32),
        "st": (n((H, S)) * u).astype(np.float32),
        "page0": (n((H, T2)) * u).astype(np.float32),
        "wgs": np.exp(0.3 * n((128, S))).astype(np.float32),
        "bonus": (0.5 * n(S2)).astype(np.float32),
        "offs": striped(np.random.permutation(T)[:S]),
        "offs2": striped(np.random.permutation(T3)[:S2]),
        "offs3": striped(np.random.permutation(T2)[:S]),
        "offs4": striped(np.random.permutation(T2)[:P]),
    }

def reference(tab_words, tab_scales, tab2_words, tab2_scales, wg_words, wg_scales,
              wb, st, page0, wgs, bonus, offs, offs2, offs3, offs4):
    v = unpack_weight(tab_words, tab_scales, "e4m3")[:, unstriped(offs)]
    v2 = unpack_weight(tab2_words, tab2_scales, "e4m3")[:, unstriped(offs2)]
    a = unpack_weight(wg_words, wg_scales, "e2m1").T @ v
    b = mxq(f64(wb), 0, "e4m3").T @ v
    x = f64(st)
    gate = 1.0 / (1.0 + np.exp(-a))
    h = x + gate * (b - x)
    page = f64(page0).copy()
    page[:, unstriped(offs3)] = np.tile(f64(wgs), (H // 128, 1)) * h
    e = v2.T @ mxq(page, 0, "e4m3")
    return e[:, unstriped(offs4)] + f64(bonus)[:, None]

@@ -1,0 +1,292 @@
+from contextlib import ExitStack
+
+import concourse.mybir as mybir
+
+K, H, T, S, T2, T3, S2, NPICK = 512, 1024, 2048, 1024, 2048, 2048, 512, 1024
+FLOPS = 2 * K * H * S * 2 + 2 * H * S2 * T2
+
+F32 = mybir.dt.float32
+BF16 = mybir.dt.bfloat16
+I32 = mybir.dt.int32
+U32 = mybir.dt.uint32
+U16 = mybir.dt.uint16
+U8 = mybir.dt.uint8
+FP8X4 = mybir.dt.float8_e4m3fn_x4
+FP4X4 = mybir.dt.float4_e2m1fn_x4
+ALU = mybir.AluOpType
+ACT = mybir.ActivationFunctionType
+
+P = 128
+PACK = 4
+BANK = 512
+SLOT_ORDER = (0, 2, 3, 1)
+PAGE_SLOTS = ("pg0", "pg1", "pg2", "pg3", "pg4", "pg0", "pg1", "pg4")
+SCORE_SLOTS = ("pg2", "pg3", "pg0", "pg1")
+
+
+def tile_list_taxi_rank_scores_kernel(
+    tc, tab_words, tab_scales, tab2_words, tab2_scales, wg_words, wg_scales,
+    wb, st, page0, wgs, bonus, offs, offs2, offs3, offs4, out,
+):
+    nc = tc.nc
+    with ExitStack() as ctx:
+        lists = ctx.enter_context(tc.tile_pool(name="lists", bufs=1))
+        keep = ctx.enter_context(tc.tile_pool(name="keep", bufs=1))
+        work = ctx.enter_context(tc.tile_pool(name="work", bufs=3))
+        psum = ctx.enter_context(tc.psum_pool(name="psum", bufs=2))
+        psum_e = ctx.enter_context(tc.psum_pool(name="psum_e", bufs=4))
+
+        def load_list(src, name):
+            tile = lists.tile([P, src.shape[1]], U16, name=name)
+            nc.sync.dma_start(tile[:], src)
+            return tile
+
+        def load_scale_rows(queue, plane, scales):
+            passes = scales.shape[0]
+            for q in range(4):
+                queue.dma_start(
+                    plane[32 * q : 32 * q + 4 * passes, :].bitcast(I32),
+                    scales[:, 4 * q : 4 * q + 4, :].bitcast(I32) if passes > 1 else scales[0, 4 * q : 4 * q + 4, :].bitcast(I32),
+                )
+
+        def load_words(words, tag):
+            tile = keep.tile([P, words.shape[1]], I32, name=tag, tag=tag, align_bytes=64)
+            nc.sync.dma_start(tile[:], words.rearrange("p n i -> p (n i)").bitcast(I32))
+            return tile
+
+        st_rows = st.rearrange("(a p t) j -> a t p j", p=P, t=PACK)
+        page_rows = page0.rearrange("(a p t) c -> a t p c", p=P, t=PACK)
+        wgs_rows = wgs.rearrange("(q t) j -> q t j", t=PACK)
+        wb_rows = wb.rearrange("(p i) r -> p i r", i=PACK)
+
+        wg_plane = keep.tile([P, H], U8, name="wg_plane", align_bytes=64)
+        tab_plane = keep.tile([P, T], U8, name="tab_plane", align_bytes=64)
+        tab2_plane = keep.tile([P, T3], U8, name="tab2_plane", align_bytes=64)
+        nc.vector.memset(wg_plane[:].bitcast(I32), 0)
+        nc.vector.memset(tab_plane[:].bitcast(I32), 0)
+        nc.gpsimd.memset(tab2_plane[:].bitcast(I32), 0)
+
+        idx = load_list(offs, "idx")
+        wg_raw = keep.tile([P, 2 * H], U8, name="wg_raw", align_bytes=64)
+        nc.sync.dma_start(wg_raw[:].bitcast(I32), wg_words[0].bitcast(I32))
+        tab_w = load_words(tab_words[0], "slot_a")
+        load_scale_rows(nc.scalar, wg_plane, wg_scales)
+        load_scale_rows(nc.scalar, tab_plane, tab_scales)
+
+        def load_wb(a, tag):
+            tile = keep.tile([P, PACK, BANK], F32, name=tag, tag=tag, align_bytes=64)
+            nc.sync.dma_start(tile[:], wb_rows[:, :, a * BANK : (a + 1) * BANK])
+            return tile
+
+        def load_state(a, t):
+            tag = f"state{slices.index((a, t))}"
+            tile = keep.tile([P, S], F32, name=tag, tag=tag, align_bytes=64)
+            nc.sync.dma_start(tile[:], st_rows[a, t])
+            return tile
+
+        def load_page(a, t):
+            tile = keep.tile([P, T2], F32, name="page", tag=PAGE_SLOTS[slices.index((a, t))])
+            nc.sync.dma_start(tile[:], page_rows[a, t])
+            return tile
+
+        def load_factors(t, queues):
+            tile = keep.tile([P, S], F32, name=f"factors{t}")
+            for q in (0, 2, 1, 3):
+                queues[q // 2].dma_start(tile[32 * q : 32 * q + 32, :], wgs_rows[:, t, :])
+            return tile
+
+        slices = [(a, t) for a in range(2) for t in SLOT_ORDER]
+        wb_raw = {0: load_wb(0, "slot_b")}
+        state = {slices[0]: load_state(*slices[0])}
+        factors = {0: load_factors(0, (nc.sync, nc.scalar))}
+        idx2 = load_list(offs2, "idx2")
+        idx3 = load_list(offs3, "idx3")
+        load_scale_rows(nc.scalar, tab2_plane, tab2_scales)
+        state[slices[1]] = load_state(*slices[1])
+        tab2_w = {0: load_words(tab2_words[0], "slot_c")}
+        wb_raw[1] = load_wb(1, "slot_e")
+        page = {slices[0]: load_page(*slices[0])}
+        for n in range(1, 5):
+            if n < PACK:
+                factors[SLOT_ORDER[n]] = load_factors(SLOT_ORDER[n], (nc.sync, nc.sync))
+            state[slices[n + 1]] = load_state(*slices[n + 1])
+            page[slices[n]] = load_page(*slices[n])
+            if n == 1:
+                tab2_w[1] = load_words(tab2_words[1], "slot_d")
+        for n in (6, 7):
+            state[slices[n]] = load_state(*slices[n])
+        idx4 = load_list(offs4, "idx4")
+        bonus_col = keep.tile([P, S2 // P], F32, name="bonus_col")
+        with nc.allow_non_contiguous_dma(reason="one value a partition"):
+            nc.sync.dma_start(bonus_col[:], bonus.rearrange("(n p) -> p n", p=P))
+
+        wg_codes = keep.tile([P, 2 * H], U8, name="wg_codes", align_bytes=64)
+        wg_sc = keep.tile([P, H], U8, name="wg_sc", align_bytes=64)
+        nc.vector.tensor_copy(
+            wg_codes[:].bitcast(U16).rearrange("p (a t m) -> p a t m", a=2, t=PACK),
+            wg_raw[:].bitcast(U16).rearrange("p (a m t) -> p a t m", a=2, t=PACK),
+        )
+        nc.vector.tensor_copy(
+            wg_sc[:].rearrange("p (a t m) -> p a t m", a=2, t=PACK),
+            wg_plane[:].rearrange("p (a m t) -> p a t m", a=2, t=PACK),
+        )
+
+        v_codes, v_sc = [], []
+        for h in range(S // BANK):
+            part = idx[:, h * BANK // 16 : (h + 1) * BANK // 16]
+            codes = keep.tile([P, BANK], U32, name=f"v_codes{h}", align_bytes=64)
+            nc.vector.tensor_copy(codes[:], tab_w[:].bitcast(U32).indirect(part))
+            sc = keep.tile([P, BANK], U8, name=f"v_sc{h}", align_bytes=64)
+            nc.vector.tensor_copy(sc[:], tab_plane[:].indirect(part))
+            v_codes.append(codes)
+            v_sc.append(sc)
+
+        wb_codes, wb_sc = {}, {}
+
+        def quantise_wb(a):
+            grouped = keep.tile([P, PACK * BANK], BF16, name="wb_grouped", tag="wb_grouped", align_bytes=64)
+            nc.scalar.copy(
+                grouped[:].rearrange("p (t m i) -> p m t i", t=PACK, i=PACK),
+                wb_raw[a][:].rearrange("p i (m t) -> p m t i", t=PACK),
+            )
+            wb_codes[a] = keep.tile([P, BANK], U32, name=f"wb_codes{a}", align_bytes=64)
+            wb_sc[a] = keep.tile([P, BANK], U8, name=f"wb_sc{a}", align_bytes=64)
+            nc.vector.quantize_mx(wb_codes[a][:].bitcast(FP8X4), wb_sc[a][:], grouped[:])
+
+        quantise_wb(0)
+
+        cab_codes = {}
+        cab_sc = keep.tile([P, S2], U8, name="cab_sc", align_bytes=64)
+
+        def gather_cabs(a):
+            cab_codes[a] = keep.tile([P, S2], U32, name=f"cab_codes{a}", align_bytes=64)
+            nc.vector.tensor_copy(cab_codes[a][:], tab2_w[a][:].bitcast(U32).indirect(idx2[:]))
+
+        def new_states(a, t, units):
+            gate = work.tile([P, S], F32, name="gate")
+            mix = work.tile([P, S], F32, name="mix")
+            x = state[(a, t)]
+            m0 = t * P
+            for h in range(S // BANK):
+                cols = slice(h * BANK, (h + 1) * BANK)
+                acc_a = psum.tile([P, BANK], F32, name="acc_a", tag="acc_a")
+                g0 = a * BANK + m0
+                nc.tensor.matmul_mx(
+                    acc_a[:], wg_codes[:, 2 * g0 : 2 * (g0 + P)].bitcast(FP4X4), wg_sc[:, g0 : g0 + P],
+                    v_codes[h][:].bitcast(FP8X4), v_sc[h][:], start=True, stop=True,
+                )
+                acc_b = psum.tile([P, BANK], F32, name="acc_b", tag="acc_b")
+                nc.tensor.matmul_mx(
+                    acc_b[:], wb_codes[a][:, m0 : m0 + P].bitcast(FP8X4), wb_sc[a][:, m0 : m0 + P],
+                    v_codes[h][:].bitcast(FP8X4), v_sc[h][:], start=True, stop=True,
+                )
+                nc.scalar.activation(gate[:, cols], acc_a[:], ACT.Sigmoid)
+                nc.vector.tensor_tensor(mix[:, cols], acc_b[:], x[:, cols], ALU.subtract)
+            width = S // units
+            for u in range(units):
+                cols = slice(u * width, (u + 1) * width)
+                nc.gpsimd.tensor_tensor(mix[:, cols], mix[:, cols], gate[:, cols], ALU.mult)
+                nc.gpsimd.tensor_tensor(mix[:, cols], mix[:, cols], x[:, cols], ALU.add)
+                nc.gpsimd.tensor_tensor(mix[:, cols], mix[:, cols], factors[t][:, cols], ALU.mult)
+            return mix
+
+        def scatter(a, t, mix, units):
+            width = S // units
+            for u in range(units):
+                part = idx3[:, u * width // 16 : (u + 1) * width // 16]
+                nc.vector.tensor_copy(page[(a, t)][:].indirect(part), mix[:, u * width : (u + 1) * width])
+
+        page_codes, page_sc = {}, {}
+        pairs = {}
+
+        def copy_on(engine, dst, src):
+            if engine == "scalar":
+                nc.scalar.copy(dst, src)
+            else:
+                nc.vector.tensor_copy(dst, src)
+
+        def round_slice(a, t, engine, cols):
+            copy_on(engine, pairs[a][:, t // 2, cols, t % 2], page[(a, t)][:, cols])
+
+        def weave(a, woven, engine, cols):
+            copy_on(
+                engine,
+                woven[:, cols, :].rearrange("p c (u i) -> p c u i", u=2),
+                pairs[a][:, :, cols, :].rearrange("p u c i -> p c u i"),
+            )
+
+        def quantise_page(a, woven, cols):
+            nc.vector.quantize_mx(
+                page_codes[a][:, cols].bitcast(FP8X4), page_sc[a][:, cols],
+                woven[:, cols, :].rearrange("p c i -> p (c i)"),
+            )
+
+        mixes = {slices[0]: new_states(*slices[0], 2)}
+        gather_cabs(0)
+        quantise_wb(1)
+        nc.vector.tensor_copy(cab_sc[:], tab2_plane[:].indirect(idx2[:]))
+        for n, (a, t) in enumerate(slices):
+            if n + 1 < len(slices):
+                mixes[slices[n + 1]] = new_states(*slices[n + 1], 1)
+            scatter(a, t, mixes[(a, t)], 2 if n == 0 else 1)
+            if n == 0:
+                gather_cabs(1)
+            if t == SLOT_ORDER[0]:
+                pairs[a] = keep.tile([P, 2, T2, 2], BF16, name="pairs", tag="pairs", align_bytes=64)
+            if n + 1 < len(slices):
+                round_slice(a, t, "scalar", slice(0, T2))
+            if n in (0, 1, 4):
+                later = {0: 5, 1: 6, 4: 7}[n]
+                page[slices[later]] = load_page(*slices[later])
+            if n == PACK - 1:
+                woven = keep.tile([P, T2, PACK], BF16, name="woven", tag="woven", align_bytes=64)
+                for c in range(2):
+                    cols = slice(c * T2 // 2, (c + 1) * T2 // 2)
+                    weave(a, woven, "scalar", cols)
+            if n == len(slices) - 2:
+                page_codes[0] = keep.tile([P, T2], U32, name="page_codes0", tag="state7", align_bytes=64)
+                page_sc[0] = keep.tile([P, T2], U8, name="page_sc0", align_bytes=64)
+                for c in range(2):
+                    quantise_page(0, woven, slice(c * T2 // 2, (c + 1) * T2 // 2))
+
+        a, t = slices[-1]
+        page_codes[a] = keep.tile([P, T2], U32, name="page_codes1", align_bytes=64)
+        page_sc[a] = keep.tile([P, T2], U8, name="page_sc1", align_bytes=64)
+        woven = keep.tile([P, T2, PACK], BF16, name="woven", tag="woven", align_bytes=64)
+        chunks = [slice(c * BANK, (c + 1) * BANK) for c in range(T2 // BANK)]
+        engines = ("vector", "vector", "scalar", "scalar")
+        for c in (0, 2, 1, 3):
+            round_slice(a, t, engines[c], chunks[c])
+            weave(a, woven, engines[c], chunks[c])
+        for c in range(T2 // BANK):
+            quantise_page(a, woven, chunks[c])
+
+        slot_tags = ("slot_a", "slot_b", "slot_c", "slot_d")
+        for n in range(S2 // P):
+            cabs = slice(n * P, (n + 1) * P)
+            scores = keep.tile([P, T2], F32, name="scores", tag=SCORE_SLOTS[n])
+            for c in range(T2 // BANK):
+                if n % 2 == 0:
+                    acc = psum_e.tile([P, BANK], F32, name="acc_e", tag="acc_e")
+                else:
+                    tag = "acc_a" if c % 2 == 0 else "acc_b"
+                    acc = psum.tile([P, BANK], F32, name=tag, tag=tag)
+                for a in range(2):
+                    nc.tensor.matmul_mx(
+                        acc[:], cab_codes[a][:, cabs].bitcast(FP8X4), cab_sc[4 * a : P, cabs],
+                        page_codes[a][:, chunks[c]].bitcast(FP8X4), page_sc[a][:, chunks[c]],
+                        start=(a == 0), stop=(a == 1),
+                    )
+                copy_on("vector" if (n == 0 and c < 2) else "scalar", scores[:, chunks[c]], acc[:])
+            picked = keep.tile([P, NPICK], F32, name="picked", tag=slot_tags[n], align_bytes=64)
+            last = n == S2 // P - 1
+            bounds = (0, 512, 768, 1024) if last else (0, 1024)
+            for lo, hi in zip(bounds, bounds[1:]):
+                nc.vector.tensor_copy(picked[:, lo:hi], scores[:].indirect(idx4[:, lo // 16 : hi // 16]))
+                if last:
+                    nc.scalar.activation(picked[:, lo:hi], picked[:, lo:hi], ACT.Identity, bias=bonus_col[:, n : n + 1])
+                else:
+                    nc.gpsimd.tensor_scalar(
+                        picked[:, lo:hi], picked[:, lo:hi], 1.0, bonus_col[:, n : n + 1], ALU.mult, ALU.add
+                    )
+                nc.sync.dma_start(out[cabs, lo:hi], picked[:, lo:hi])

@@ -20,6 +20,8 @@ P = 128
 PACK = 4
 BANK = 512
 SLOT_ORDER = (0, 2, 3, 1)
+UNITS = ((0, 512, 1024),) + ((0, 1024),) * 6 + ((0, 512, 1024),)
+GPSIMD_SUBTRACTS = (4,)
 PAGE_SLOTS = ("pg0", "pg1", "pg2", "pg3", "pg4", "pg0", "pg1", "pg4")
 SCORE_SLOTS = ("pg2", "pg3", "pg0", "pg1")
 
@@ -62,17 +64,17 @@ def tile_list_taxi_rank_scores_kernel(
         wg_plane = keep.tile([P, H], U8, name="wg_plane", align_bytes=64)
         tab_plane = keep.tile([P, T], U8, name="tab_plane", align_bytes=64)
         tab2_plane = keep.tile([P, T3], U8, name="tab2_plane", align_bytes=64)
-        nc.vector.memset(wg_plane[:].bitcast(I32), 0)
         nc.vector.memset(tab_plane[:].bitcast(I32), 0)
+        nc.gpsimd.memset(wg_plane[:].bitcast(I32), 0)
         nc.gpsimd.memset(tab2_plane[:].bitcast(I32), 0)
 
         idx = load_list(offs, "idx")
         wg_raw = keep.tile([P, 2 * H], U8, name="wg_raw", align_bytes=64)
         nc.sync.dma_start(wg_raw[:].bitcast(I32), wg_words[0].bitcast(I32))
+        idx2 = load_list(offs2, "idx2")
+        idx3 = load_list(offs3, "idx3")
         tab_w = load_words(tab_words[0], "slot_a")
-        load_scale_rows(nc.scalar, wg_plane, wg_scales)
-        load_scale_rows(nc.scalar, tab_plane, tab_scales)
-
+        load_scale_rows(nc.sync, tab_plane, tab_scales)
         def load_wb(a, tag):
             tile = keep.tile([P, PACK, BANK], F32, name=tag, tag=tag, align_bytes=64)
             nc.sync.dma_start(tile[:], wb_rows[:, :, a * BANK : (a + 1) * BANK])
@@ -97,24 +99,24 @@ def tile_list_taxi_rank_scores_kernel(
 
         slices = [(a, t) for a in range(2) for t in SLOT_ORDER]
         wb_raw = {0: load_wb(0, "slot_b")}
-        state = {slices[0]: load_state(*slices[0])}
-        factors = {0: load_factors(0, (nc.sync, nc.scalar))}
-        idx2 = load_list(offs2, "idx2")
-        idx3 = load_list(offs3, "idx3")
-        load_scale_rows(nc.scalar, tab2_plane, tab2_scales)
-        state[slices[1]] = load_state(*slices[1])
-        tab2_w = {0: load_words(tab2_words[0], "slot_c")}
+        load_scale_rows(nc.sync, wg_plane, wg_scales)
+        first_states = keep.tile([P, 2, S], F32, name="first_states", align_bytes=64)
+        nc.sync.dma_start(first_states[:], st.rearrange("(a p u v) j -> a v p u j", p=P, u=2, v=2)[0, 0])
+        state = {slices[0]: first_states[:, 0, :], slices[1]: first_states[:, 1, :]}
+        factors = {0: load_factors(0, (nc.sync, nc.sync))}
         wb_raw[1] = load_wb(1, "slot_e")
         page = {slices[0]: load_page(*slices[0])}
+        state[slices[2]] = load_state(*slices[2])
+        load_scale_rows(nc.sync, tab2_plane, tab2_scales)
+        tab2_w = {0: load_words(tab2_words[0], "slot_c")}
         for n in range(1, 5):
             if n < PACK:
                 factors[SLOT_ORDER[n]] = load_factors(SLOT_ORDER[n], (nc.sync, nc.sync))
-            state[slices[n + 1]] = load_state(*slices[n + 1])
+            state[slices[n + 2]] = load_state(*slices[n + 2])
             page[slices[n]] = load_page(*slices[n])
             if n == 1:
                 tab2_w[1] = load_words(tab2_words[1], "slot_d")
-        for n in (6, 7):
-            state[slices[n]] = load_state(*slices[n])
+        state[slices[7]] = load_state(*slices[7])
         idx4 = load_list(offs4, "idx4")
         bonus_col = keep.tile([P, S2 // P], F32, name="bonus_col")
         with nc.allow_non_contiguous_dma(reason="one value a partition"):
@@ -143,28 +145,43 @@ def tile_list_taxi_rank_scores_kernel(
 
         wb_codes, wb_sc = {}, {}
 
-        def quantise_wb(a):
-            grouped = keep.tile([P, PACK * BANK], BF16, name="wb_grouped", tag="wb_grouped", align_bytes=64)
+        def quantise_wb(a, t0, t1):
+            slots = t1 - t0
+            tag = f"wb_grouped{slots}"
+            grouped = keep.tile([P, slots * BANK], BF16, name=tag, tag=tag, align_bytes=64)
             nc.scalar.copy(
-                grouped[:].rearrange("p (t m i) -> p m t i", t=PACK, i=PACK),
-                wb_raw[a][:].rearrange("p i (m t) -> p m t i", t=PACK),
+                grouped[:].rearrange("p (t m i) -> p m t i", t=slots, i=PACK),
+                wb_raw[a][:].rearrange("p i (m t) -> p m t i", t=PACK)[:, :, t0:t1, :],
             )
-            wb_codes[a] = keep.tile([P, BANK], U32, name=f"wb_codes{a}", align_bytes=64)
-            wb_sc[a] = keep.tile([P, BANK], U8, name=f"wb_sc{a}", align_bytes=64)
-            nc.vector.quantize_mx(wb_codes[a][:].bitcast(FP8X4), wb_sc[a][:], grouped[:])
+            codes_tag = f"wb_codes{a}{t0}"
+            codes = keep.tile([P, slots * P], U32, name=codes_tag, tag=codes_tag, align_bytes=64)
+            sc = keep.tile([P, slots * P], U8, name=f"wb_sc{a}{t0}", align_bytes=64)
+            nc.vector.quantize_mx(codes[:].bitcast(FP8X4), sc[:], grouped[:])
+            for t in range(t0, t1):
+                cols = slice((t - t0) * P, (t - t0 + 1) * P)
+                wb_codes[(a, t)] = codes[:, cols]
+                wb_sc[(a, t)] = sc[:, cols]
 
-        quantise_wb(0)
+        quantise_wb(0, 0, 1)
+        quantise_wb(0, 2, 4)
+        quantise_wb(0, 1, 2)
 
-        cab_codes = {}
-        cab_sc = keep.tile([P, S2], U8, name="cab_sc", align_bytes=64)
+        cab_codes, cab_sc = {}, {}
+        half = S2 // 2
 
-        def gather_cabs(a):
-            cab_codes[a] = keep.tile([P, S2], U32, name=f"cab_codes{a}", align_bytes=64)
-            nc.vector.tensor_copy(cab_codes[a][:], tab2_w[a][:].bitcast(U32).indirect(idx2[:]))
+        def gather_cab_words(a, h, tag):
+            cab_codes[(a, h)] = keep.tile([P, half], U32, name=tag, tag=tag, align_bytes=64)
+            part = idx2[:, h * half // 16 : (h + 1) * half // 16]
+            nc.vector.tensor_copy(cab_codes[(a, h)][:], tab2_w[a][:].bitcast(U32).indirect(part))
+
+        def gather_cab_scales(h, tag):
+            cab_sc[h] = keep.tile([P, half], U8, name=tag, tag=tag, align_bytes=64)
+            part = idx2[:, h * half // 16 : (h + 1) * half // 16]
+            nc.vector.tensor_copy(cab_sc[h][:], tab2_plane[:].indirect(part))
 
         def new_states(a, t, units):
             gate = work.tile([P, S], F32, name="gate")
-            mix = work.tile([P, S], F32, name="mix")
+            mix = keep.tile([P, S], F32, name="mix", tag=f"mix{slices.index((a, t)) % 3}", align_bytes=64)
             x = state[(a, t)]
             m0 = t * P
             for h in range(S // BANK):
@@ -177,24 +194,35 @@ def tile_list_taxi_rank_scores_kernel(
                 )
                 acc_b = psum.tile([P, BANK], F32, name="acc_b", tag="acc_b")
                 nc.tensor.matmul_mx(
-                    acc_b[:], wb_codes[a][:, m0 : m0 + P].bitcast(FP8X4), wb_sc[a][:, m0 : m0 + P],
+                    acc_b[:], wb_codes[(a, t)].bitcast(FP8X4), wb_sc[(a, t)],
                     v_codes[h][:].bitcast(FP8X4), v_sc[h][:], start=True, stop=True,
                 )
                 nc.scalar.activation(gate[:, cols], acc_a[:], ACT.Sigmoid)
-                nc.vector.tensor_tensor(mix[:, cols], acc_b[:], x[:, cols], ALU.subtract)
-            width = S // units
-            for u in range(units):
-                cols = slice(u * width, (u + 1) * width)
-                nc.gpsimd.tensor_tensor(mix[:, cols], mix[:, cols], gate[:, cols], ALU.mult)
-                nc.gpsimd.tensor_tensor(mix[:, cols], mix[:, cols], x[:, cols], ALU.add)
-                nc.gpsimd.tensor_tensor(mix[:, cols], mix[:, cols], factors[t][:, cols], ALU.mult)
+                if slices.index((a, t)) in GPSIMD_SUBTRACTS:
+                    nc.scalar.copy(mix[:, cols], acc_b[:])
+                else:
+                    nc.vector.tensor_tensor(mix[:, cols], acc_b[:], x[:, cols], ALU.subtract)
+                if (a, t) == slices[0] and h == 0:
+                    nc.vector.tensor_tensor(mix[:, cols], mix[:, cols], gate[:, cols], ALU.mult)
+                    nc.vector.tensor_tensor(mix[:, cols], mix[:, cols], x[:, cols], ALU.add)
+                    nc.vector.tensor_tensor(mix[:, cols], mix[:, cols], factors[t][:, cols], ALU.mult)
+            for lo, hi in zip(units, units[1:]):
+                if (a, t) == slices[0] and lo == 0:
+                    continue
+                cols = slice(lo, hi)
+                blend = keep.tile([P, hi - lo], F32, name="blend", tag="blend", align_bytes=64)
+                if slices.index((a, t)) in GPSIMD_SUBTRACTS:
+                    nc.gpsimd.tensor_tensor(blend[:], mix[:, cols], x[:, cols], ALU.subtract)
+                    nc.gpsimd.tensor_tensor(blend[:], blend[:], gate[:, cols], ALU.mult)
+                else:
+                    nc.gpsimd.tensor_tensor(blend[:], mix[:, cols], gate[:, cols], ALU.mult)
+                nc.gpsimd.tensor_tensor(blend[:], blend[:], x[:, cols], ALU.add)
+                nc.gpsimd.tensor_tensor(mix[:, cols], blend[:], factors[t][:, cols], ALU.mult)
             return mix
 
         def scatter(a, t, mix, units):
-            width = S // units
-            for u in range(units):
-                part = idx3[:, u * width // 16 : (u + 1) * width // 16]
-                nc.vector.tensor_copy(page[(a, t)][:].indirect(part), mix[:, u * width : (u + 1) * width])
+            for lo, hi in zip(units, units[1:]):
+                nc.vector.tensor_copy(page[(a, t)][:].indirect(idx3[:, lo // 16 : hi // 16]), mix[:, lo:hi])
 
         page_codes, page_sc = {}, {}
         pairs = {}
@@ -208,29 +236,31 @@ def tile_list_taxi_rank_scores_kernel(
         def round_slice(a, t, engine, cols):
             copy_on(engine, pairs[a][:, t // 2, cols, t % 2], page[(a, t)][:, cols])
 
-        def weave(a, woven, engine, cols):
+        def weave(a, engine, cols, tag):
+            woven = keep.tile([P, cols.stop - cols.start, PACK], BF16, name="woven", tag=tag, align_bytes=64)
             copy_on(
                 engine,
-                woven[:, cols, :].rearrange("p c (u i) -> p c u i", u=2),
+                woven[:].rearrange("p c (u i) -> p c u i", u=2),
                 pairs[a][:, :, cols, :].rearrange("p u c i -> p c u i"),
             )
+            return woven
 
         def quantise_page(a, woven, cols):
             nc.vector.quantize_mx(
                 page_codes[a][:, cols].bitcast(FP8X4), page_sc[a][:, cols],
-                woven[:, cols, :].rearrange("p c i -> p (c i)"),
+                woven[:].rearrange("p c i -> p (c i)"),
             )
 
-        mixes = {slices[0]: new_states(*slices[0], 2)}
-        gather_cabs(0)
-        quantise_wb(1)
-        nc.vector.tensor_copy(cab_sc[:], tab2_plane[:].indirect(idx2[:]))
+        mixes = {slices[0]: new_states(*slices[0], UNITS[0])}
+        quantise_wb(1, 0, PACK)
+        gather_cab_words(0, 0, "cab_codes0")
+        gather_cab_scales(0, "cab_sc")
         for n, (a, t) in enumerate(slices):
             if n + 1 < len(slices):
-                mixes[slices[n + 1]] = new_states(*slices[n + 1], 1)
-            scatter(a, t, mixes[(a, t)], 2 if n == 0 else 1)
+                mixes[slices[n + 1]] = new_states(*slices[n + 1], UNITS[n + 1])
+            scatter(a, t, mixes[(a, t)], UNITS[n])
             if n == 0:
-                gather_cabs(1)
+                gather_cab_words(1, 0, "cab_codes1")
             if t == SLOT_ORDER[0]:
                 pairs[a] = keep.tile([P, 2, T2, 2], BF16, name="pairs", tag="pairs", align_bytes=64)
             if n + 1 < len(slices):
@@ -239,31 +269,34 @@ def tile_list_taxi_rank_scores_kernel(
                 later = {0: 5, 1: 6, 4: 7}[n]
                 page[slices[later]] = load_page(*slices[later])
             if n == PACK - 1:
-                woven = keep.tile([P, T2, PACK], BF16, name="woven", tag="woven", align_bytes=64)
-                for c in range(2):
-                    cols = slice(c * T2 // 2, (c + 1) * T2 // 2)
-                    weave(a, woven, "scalar", cols)
-            if n == len(slices) - 2:
-                page_codes[0] = keep.tile([P, T2], U32, name="page_codes0", tag="state7", align_bytes=64)
-                page_sc[0] = keep.tile([P, T2], U8, name="page_sc0", align_bytes=64)
-                for c in range(2):
-                    quantise_page(0, woven, slice(c * T2 // 2, (c + 1) * T2 // 2))
+                halves = [slice(c * T2 // 2, (c + 1) * T2 // 2) for c in range(2)]
+                woven_first = [weave(a, "scalar", cols, tag) for cols, tag in zip(halves, ("slot_b", "slot_e"))]
+
+        page_codes[0] = keep.tile([P, T2], U32, name="page_codes0", align_bytes=64)
+        page_sc[0] = keep.tile([P, T2], U8, name="page_sc0", tag="mix1", align_bytes=64)
+        for woven, cols in zip(woven_first, halves):
+            quantise_page(0, woven, cols)
 
         a, t = slices[-1]
         page_codes[a] = keep.tile([P, T2], U32, name="page_codes1", align_bytes=64)
         page_sc[a] = keep.tile([P, T2], U8, name="page_sc1", align_bytes=64)
-        woven = keep.tile([P, T2, PACK], BF16, name="woven", tag="woven", align_bytes=64)
         chunks = [slice(c * BANK, (c + 1) * BANK) for c in range(T2 // BANK)]
-        engines = ("vector", "vector", "scalar", "scalar")
-        for c in (0, 2, 1, 3):
-            round_slice(a, t, engines[c], chunks[c])
-            weave(a, woven, engines[c], chunks[c])
+        engines = ("scalar", "scalar", "vector", "vector")
+        woven_last = []
         for c in range(T2 // BANK):
-            quantise_page(a, woven, chunks[c])
+            round_slice(a, t, engines[c], chunks[c])
+            woven_last.append(weave(a, engines[c], chunks[c], f"state{2 + c}"))
+        for c in range(T2 // BANK):
+            quantise_page(a, woven_last[c], chunks[c])
 
-        slot_tags = ("slot_a", "slot_b", "slot_c", "slot_d")
+        gather_cab_words(0, 1, "state4")
+        gather_cab_words(1, 1, "state5")
+        gather_cab_scales(1, "state3")
+
+        slot_tags = ("slot_a", "slot_b", "slot_e", "state6")
         for n in range(S2 // P):
             cabs = slice(n * P, (n + 1) * P)
+            own = slice(n % 2 * P, (n % 2 + 1) * P)
             scores = keep.tile([P, T2], F32, name="scores", tag=SCORE_SLOTS[n])
             for c in range(T2 // BANK):
                 if n % 2 == 0:
@@ -273,11 +306,11 @@ def tile_list_taxi_rank_scores_kernel(
                     acc = psum.tile([P, BANK], F32, name=tag, tag=tag)
                 for a in range(2):
                     nc.tensor.matmul_mx(
-                        acc[:], cab_codes[a][:, cabs].bitcast(FP8X4), cab_sc[4 * a : P, cabs],
+                        acc[:], cab_codes[(a, n // 2)][:, own].bitcast(FP8X4), cab_sc[n // 2][4 * a : P, own],
                         page_codes[a][:, chunks[c]].bitcast(FP8X4), page_sc[a][:, chunks[c]],
                         start=(a == 0), stop=(a == 1),
                     )
-                copy_on("vector" if (n == 0 and c < 2) else "scalar", scores[:, chunks[c]], acc[:])
+                nc.scalar.copy(scores[:, chunks[c]], acc[:])
             picked = keep.tile([P, NPICK], F32, name="picked", tag=slot_tags[n], align_bytes=64)
             last = n == S2 // P - 1
             bounds = (0, 512, 768, 1024) if last else (0, 1024)

@@ -21,7 +21,7 @@ PACK = 4
 BANK = 512
 SLOT_ORDER = (0, 2, 3, 1)
 UNITS = ((0, 512, 1024),) + ((0, 1024),) * 6 + ((0, 512, 1024),)
-GPSIMD_SUBTRACTS = (4,)
+GPSIMD_SUBTRACTS = ()
 PAGE_SLOTS = ("pg0", "pg1", "pg2", "pg3", "pg4", "pg0", "pg1", "pg4")
 SCORE_SLOTS = ("pg2", "pg3", "pg0", "pg1")
 
@@ -91,32 +91,32 @@ def tile_list_taxi_rank_scores_kernel(
             nc.sync.dma_start(tile[:], page_rows[a, t])
             return tile
 
-        def load_factors(t, queues):
-            tile = keep.tile([P, S], F32, name=f"factors{t}")
+        factors = {}
+
+        def load_factors(t, cols):
+            if t not in factors:
+                factors[t] = keep.tile([P, S], F32, name=f"factors{t}")
             for q in (0, 2, 1, 3):
-                queues[q // 2].dma_start(tile[32 * q : 32 * q + 32, :], wgs_rows[:, t, :])
-            return tile
+                nc.sync.dma_start(factors[t][32 * q : 32 * q + 32, cols], wgs_rows[:, t, cols])
 
         slices = [(a, t) for a in range(2) for t in SLOT_ORDER]
         wb_raw = {0: load_wb(0, "slot_b")}
         load_scale_rows(nc.sync, wg_plane, wg_scales)
-        first_states = keep.tile([P, 2, S], F32, name="first_states", align_bytes=64)
-        nc.sync.dma_start(first_states[:], st.rearrange("(a p u v) j -> a v p u j", p=P, u=2, v=2)[0, 0])
-        state = {slices[0]: first_states[:, 0, :], slices[1]: first_states[:, 1, :]}
-        factors = {0: load_factors(0, (nc.sync, nc.sync))}
-        wb_raw[1] = load_wb(1, "slot_e")
+        state = {slices[0]: load_state(*slices[0])}
+        load_factors(SLOT_ORDER[0], slice(0, BANK))
         page = {slices[0]: load_page(*slices[0])}
+        state[slices[1]] = load_state(*slices[1])
+        load_factors(SLOT_ORDER[0], slice(BANK, S))
         state[slices[2]] = load_state(*slices[2])
-        load_scale_rows(nc.sync, tab2_plane, tab2_scales)
-        tab2_w = {0: load_words(tab2_words[0], "slot_c")}
+        wb_raw[1] = load_wb(1, "pairs")
         for n in range(1, 5):
             if n < PACK:
-                factors[SLOT_ORDER[n]] = load_factors(SLOT_ORDER[n], (nc.sync, nc.sync))
+                load_factors(SLOT_ORDER[n], slice(0, S))
             state[slices[n + 2]] = load_state(*slices[n + 2])
             page[slices[n]] = load_page(*slices[n])
-            if n == 1:
-                tab2_w[1] = load_words(tab2_words[1], "slot_d")
         state[slices[7]] = load_state(*slices[7])
+        load_scale_rows(nc.sync, tab2_plane, tab2_scales)
+        tab2_w = {0: load_words(tab2_words[0], "slot_c"), 1: load_words(tab2_words[1], "slot_d")}
         idx4 = load_list(offs4, "idx4")
         bonus_col = keep.tile([P, S2 // P], F32, name="bonus_col")
         with nc.allow_non_contiguous_dma(reason="one value a partition"):
@@ -128,10 +128,11 @@ def tile_list_taxi_rank_scores_kernel(
             wg_codes[:].bitcast(U16).rearrange("p (a t m) -> p a t m", a=2, t=PACK),
             wg_raw[:].bitcast(U16).rearrange("p (a m t) -> p a t m", a=2, t=PACK),
         )
-        nc.vector.tensor_copy(
-            wg_sc[:].rearrange("p (a t m) -> p a t m", a=2, t=PACK),
-            wg_plane[:].rearrange("p (a m t) -> p a t m", a=2, t=PACK),
-        )
+        sc_to = wg_sc[:].rearrange("p (a t m) -> p a t m", a=2, t=PACK)
+        sc_from = wg_plane[:].rearrange("p (a m t) -> p a t m", a=2, t=PACK)
+        nc.vector.tensor_copy(sc_to[:, 0, 0, :], sc_from[:, 0, 0, :])
+        nc.gpsimd.tensor_copy(sc_to[:, 0, 1:PACK, :], sc_from[:, 0, 1:PACK, :])
+        nc.gpsimd.tensor_copy(sc_to[:, 1], sc_from[:, 1])
 
         v_codes, v_sc = [], []
         for h in range(S // BANK):
@@ -253,14 +254,14 @@ def tile_list_taxi_rank_scores_kernel(
 
         mixes = {slices[0]: new_states(*slices[0], UNITS[0])}
         quantise_wb(1, 0, PACK)
-        gather_cab_words(0, 0, "cab_codes0")
-        gather_cab_scales(0, "cab_sc")
         for n, (a, t) in enumerate(slices):
             if n + 1 < len(slices):
                 mixes[slices[n + 1]] = new_states(*slices[n + 1], UNITS[n + 1])
             scatter(a, t, mixes[(a, t)], UNITS[n])
-            if n == 0:
+            if n == PACK:
+                gather_cab_words(0, 0, "cab_codes0")
                 gather_cab_words(1, 0, "cab_codes1")
+                gather_cab_scales(0, "cab_sc")
             if t == SLOT_ORDER[0]:
                 pairs[a] = keep.tile([P, 2, T2, 2], BF16, name="pairs", tag="pairs", align_bytes=64)
             if n + 1 < len(slices):
@@ -270,7 +271,7 @@ def tile_list_taxi_rank_scores_kernel(
                 page[slices[later]] = load_page(*slices[later])
             if n == PACK - 1:
                 halves = [slice(c * T2 // 2, (c + 1) * T2 // 2) for c in range(2)]
-                woven_first = [weave(a, "scalar", cols, tag) for cols, tag in zip(halves, ("slot_b", "slot_e"))]
+                woven_first = [weave(a, "scalar", cols, tag) for cols, tag in zip(halves, ("slot_a", "slot_b"))]
 
         page_codes[0] = keep.tile([P, T2], U32, name="page_codes0", align_bytes=64)
         page_sc[0] = keep.tile([P, T2], U8, name="page_sc0", tag="mix1", align_bytes=64)
@@ -293,7 +294,7 @@ def tile_list_taxi_rank_scores_kernel(
         gather_cab_words(1, 1, "state5")
         gather_cab_scales(1, "state3")
 
-        slot_tags = ("slot_a", "slot_b", "slot_e", "state6")
+        slot_tags = ("slot_a", "slot_b", "state6", "state7")
         for n in range(S2 // P):
             cabs = slice(n * P, (n + 1) * P)
             own = slice(n % 2 * P, (n % 2 + 1) * P)

@@ -21,7 +21,6 @@ PACK = 4
 BANK = 512
 SLOT_ORDER = (0, 2, 3, 1)
 UNITS = ((0, 512, 1024),) + ((0, 1024),) * 6 + ((0, 512, 1024),)
-GPSIMD_SUBTRACTS = ()
 PAGE_SLOTS = ("pg0", "pg1", "pg2", "pg3", "pg4", "pg0", "pg1", "pg4")
 SCORE_SLOTS = ("pg2", "pg3", "pg0", "pg1")
 
@@ -180,6 +179,14 @@ def tile_list_taxi_rank_scores_kernel(
             part = idx2[:, h * half // 16 : (h + 1) * half // 16]
             nc.vector.tensor_copy(cab_sc[h][:], tab2_plane[:].indirect(part))
 
+        def blend_states(engine, t, mix, gate, x, cols, with_factors):
+            blend = keep.tile([P, cols.stop - cols.start], F32, name="blend", tag="blend", align_bytes=64)
+            engine.tensor_tensor(blend[:], mix[:, cols], gate[:, cols], ALU.mult)
+            engine.tensor_tensor(blend[:], x[:, cols], blend[:], ALU.subtract)
+            if with_factors:
+                engine.tensor_tensor(mix[:, cols], blend[:], factors[t][:, cols], ALU.mult)
+            return blend
+
         def new_states(a, t, units):
             gate = work.tile([P, S], F32, name="gate")
             mix = keep.tile([P, S], F32, name="mix", tag=f"mix{slices.index((a, t)) % 3}", align_bytes=64)
@@ -199,31 +206,23 @@ def tile_list_taxi_rank_scores_kernel(
                     v_codes[h][:].bitcast(FP8X4), v_sc[h][:], start=True, stop=True,
                 )
                 nc.scalar.activation(gate[:, cols], acc_a[:], ACT.Sigmoid)
-                if slices.index((a, t)) in GPSIMD_SUBTRACTS:
-                    nc.scalar.copy(mix[:, cols], acc_b[:])
-                else:
-                    nc.vector.tensor_tensor(mix[:, cols], acc_b[:], x[:, cols], ALU.subtract)
+                nc.vector.tensor_tensor(mix[:, cols], x[:, cols], acc_b[:], ALU.subtract)
                 if (a, t) == slices[0] and h == 0:
-                    nc.vector.tensor_tensor(mix[:, cols], mix[:, cols], gate[:, cols], ALU.mult)
-                    nc.vector.tensor_tensor(mix[:, cols], mix[:, cols], x[:, cols], ALU.add)
-                    nc.vector.tensor_tensor(mix[:, cols], mix[:, cols], factors[t][:, cols], ALU.mult)
+                    blend_states(nc.vector, t, mix, gate, x, cols, True)
+            blend = None
             for lo, hi in zip(units, units[1:]):
-                if (a, t) == slices[0] and lo == 0:
-                    continue
-                cols = slice(lo, hi)
-                blend = keep.tile([P, hi - lo], F32, name="blend", tag="blend", align_bytes=64)
-                if slices.index((a, t)) in GPSIMD_SUBTRACTS:
-                    nc.gpsimd.tensor_tensor(blend[:], mix[:, cols], x[:, cols], ALU.subtract)
-                    nc.gpsimd.tensor_tensor(blend[:], blend[:], gate[:, cols], ALU.mult)
-                else:
-                    nc.gpsimd.tensor_tensor(blend[:], mix[:, cols], gate[:, cols], ALU.mult)
-                nc.gpsimd.tensor_tensor(blend[:], blend[:], x[:, cols], ALU.add)
-                nc.gpsimd.tensor_tensor(mix[:, cols], blend[:], factors[t][:, cols], ALU.mult)
-            return mix
+                if (a, t) != slices[0] or lo > 0:
+                    with_factors = (a, t) != slices[-1] or hi < S
+                    blend = blend_states(nc.gpsimd, t, mix, gate, x, slice(lo, hi), with_factors)
+            return mix, blend
 
-        def scatter(a, t, mix, units):
+        def scatter(a, t, mix, blend, units):
             for lo, hi in zip(units, units[1:]):
-                nc.vector.tensor_copy(page[(a, t)][:].indirect(idx3[:, lo // 16 : hi // 16]), mix[:, lo:hi])
+                window = page[(a, t)][:].indirect(idx3[:, lo // 16 : hi // 16])
+                if (a, t) == slices[-1] and hi == S:
+                    nc.vector.tensor_tensor(window, blend[:], factors[t][:, lo:hi], ALU.mult)
+                else:
+                    nc.vector.tensor_copy(window, mix[:, lo:hi])
 
         page_codes, page_sc = {}, {}
         pairs = {}
@@ -257,7 +256,7 @@ def tile_list_taxi_rank_scores_kernel(
         for n, (a, t) in enumerate(slices):
             if n + 1 < len(slices):
                 mixes[slices[n + 1]] = new_states(*slices[n + 1], UNITS[n + 1])
-            scatter(a, t, mixes[(a, t)], UNITS[n])
+            scatter(a, t, *mixes[(a, t)], UNITS[n])
             if n == PACK:
                 gather_cab_words(0, 0, "cab_codes0")
                 gather_cab_words(1, 0, "cab_codes1")
@@ -274,7 +273,7 @@ def tile_list_taxi_rank_scores_kernel(
                 woven_first = [weave(a, "scalar", cols, tag) for cols, tag in zip(halves, ("slot_a", "slot_b"))]
 
         page_codes[0] = keep.tile([P, T2], U32, name="page_codes0", align_bytes=64)
-        page_sc[0] = keep.tile([P, T2], U8, name="page_sc0", tag="mix1", align_bytes=64)
+        page_sc[0] = keep.tile([P, T2], U8, name="page_sc0", tag="blend", align_bytes=64)
         for woven, cols in zip(woven_first, halves):
             quantise_page(0, woven, cols)
 

from contextlib import ExitStack

import concourse.mybir as mybir

K, H, T, S, T2, T3, S2, NPICK = 512, 1024, 2048, 1024, 2048, 2048, 512, 1024
FLOPS = 2 * K * H * S * 2 + 2 * H * S2 * T2

F32 = mybir.dt.float32
BF16 = mybir.dt.bfloat16
I32 = mybir.dt.int32
U32 = mybir.dt.uint32
U16 = mybir.dt.uint16
U8 = mybir.dt.uint8
FP8X4 = mybir.dt.float8_e4m3fn_x4
FP4X4 = mybir.dt.float4_e2m1fn_x4
ALU = mybir.AluOpType
ACT = mybir.ActivationFunctionType

P = 128
PACK = 4
BANK = 512
SLOT_ORDER = (0, 2, 3, 1)
UNITS = ((0, 512, 1024),) + ((0, 1024),) * 6 + ((0, 512, 1024),)
PAGE_SLOTS = ("pg0", "pg1", "pg2", "pg3", "pg4", "pg0", "pg1", "pg4")
SCORE_SLOTS = ("pg2", "pg3", "pg0", "pg1")


def tile_list_taxi_rank_scores_kernel(
    tc, tab_words, tab_scales, tab2_words, tab2_scales, wg_words, wg_scales,
    wb, st, page0, wgs, bonus, offs, offs2, offs3, offs4, out,
):
    nc = tc.nc
    with ExitStack() as ctx:
        lists = ctx.enter_context(tc.tile_pool(name="lists", bufs=1))
        keep = ctx.enter_context(tc.tile_pool(name="keep", bufs=1))
        work = ctx.enter_context(tc.tile_pool(name="work", bufs=3))
        psum = ctx.enter_context(tc.psum_pool(name="psum", bufs=2))
        psum_e = ctx.enter_context(tc.psum_pool(name="psum_e", bufs=4))

        def load_list(src, name):
            tile = lists.tile([P, src.shape[1]], U16, name=name)
            nc.sync.dma_start(tile[:], src)
            return tile

        def load_scale_rows(queue, plane, scales):
            passes = scales.shape[0]
            for q in range(4):
                queue.dma_start(
                    plane[32 * q : 32 * q + 4 * passes, :].bitcast(I32),
                    scales[:, 4 * q : 4 * q + 4, :].bitcast(I32) if passes > 1 else scales[0, 4 * q : 4 * q + 4, :].bitcast(I32),
                )

        def load_words(words, tag):
            tile = keep.tile([P, words.shape[1]], I32, name=tag, tag=tag, align_bytes=64)
            nc.sync.dma_start(tile[:], words.rearrange("p n i -> p (n i)").bitcast(I32))
            return tile

        st_rows = st.rearrange("(a p t) j -> a t p j", p=P, t=PACK)
        page_rows = page0.rearrange("(a p t) c -> a t p c", p=P, t=PACK)
        wgs_rows = wgs.rearrange("(q t) j -> q t j", t=PACK)
        wb_rows = wb.rearrange("(p i) r -> p i r", i=PACK)

        wg_plane = keep.tile([P, H], U8, name="wg_plane", align_bytes=64)
        tab_plane = keep.tile([P, T], U8, name="tab_plane", align_bytes=64)
        tab2_plane = keep.tile([P, T3], U8, name="tab2_plane", align_bytes=64)
        nc.vector.memset(tab_plane[:].bitcast(I32), 0)
        nc.gpsimd.memset(wg_plane[:].bitcast(I32), 0)
        nc.gpsimd.memset(tab2_plane[:].bitcast(I32), 0)

        idx = load_list(offs, "idx")
        wg_raw = keep.tile([P, 2 * H], U8, name="wg_raw", align_bytes=64)
        nc.sync.dma_start(wg_raw[:].bitcast(I32), wg_words[0].bitcast(I32))
        idx2 = load_list(offs2, "idx2")
        idx3 = load_list(offs3, "idx3")
        tab_w = load_words(tab_words[0], "slot_a")
        load_scale_rows(nc.sync, tab_plane, tab_scales)
        def load_wb(a, tag):
            tile = keep.tile([P, PACK, BANK], F32, name=tag, tag=tag, align_bytes=64)
            nc.sync.dma_start(tile[:], wb_rows[:, :, a * BANK : (a + 1) * BANK])
            return tile

        def load_state(a, t):
            tag = f"state{slices.index((a, t))}"
            tile = keep.tile([P, S], F32, name=tag, tag=tag, align_bytes=64)
            nc.sync.dma_start(tile[:], st_rows[a, t])
            return tile

        def load_page(a, t):
            tile = keep.tile([P, T2], F32, name="page", tag=PAGE_SLOTS[slices.index((a, t))])
            nc.sync.dma_start(tile[:], page_rows[a, t])
            return tile

        factors = {}

        def load_factors(t, cols):
            if t not in factors:
                factors[t] = keep.tile([P, S], F32, name=f"factors{t}")
            for q in (0, 2, 1, 3):
                nc.sync.dma_start(factors[t][32 * q : 32 * q + 32, cols], wgs_rows[:, t, cols])

        slices = [(a, t) for a in range(2) for t in SLOT_ORDER]
        wb_raw = {0: load_wb(0, "slot_b")}
        load_scale_rows(nc.sync, wg_plane, wg_scales)
        state = {slices[0]: load_state(*slices[0])}
        load_factors(SLOT_ORDER[0], slice(0, BANK))
        page = {slices[0]: load_page(*slices[0])}
        state[slices[1]] = load_state(*slices[1])
        load_factors(SLOT_ORDER[0], slice(BANK, S))
        state[slices[2]] = load_state(*slices[2])
        wb_raw[1] = load_wb(1, "pairs")
        for n in range(1, 5):
            if n < PACK:
                load_factors(SLOT_ORDER[n], slice(0, S))
            state[slices[n + 2]] = load_state(*slices[n + 2])
            page[slices[n]] = load_page(*slices[n])
        state[slices[7]] = load_state(*slices[7])
        load_scale_rows(nc.sync, tab2_plane, tab2_scales)
        tab2_w = {0: load_words(tab2_words[0], "slot_c"), 1: load_words(tab2_words[1], "slot_d")}
        idx4 = load_list(offs4, "idx4")
        bonus_col = keep.tile([P, S2 // P], F32, name="bonus_col")
        with nc.allow_non_contiguous_dma(reason="one value a partition"):
            nc.sync.dma_start(bonus_col[:], bonus.rearrange("(n p) -> p n", p=P))

        wg_codes = keep.tile([P, 2 * H], U8, name="wg_codes", align_bytes=64)
        wg_sc = keep.tile([P, H], U8, name="wg_sc", align_bytes=64)
        nc.vector.tensor_copy(
            wg_codes[:].bitcast(U16).rearrange("p (a t m) -> p a t m", a=2, t=PACK),
            wg_raw[:].bitcast(U16).rearrange("p (a m t) -> p a t m", a=2, t=PACK),
        )
        sc_to = wg_sc[:].rearrange("p (a t m) -> p a t m", a=2, t=PACK)
        sc_from = wg_plane[:].rearrange("p (a m t) -> p a t m", a=2, t=PACK)
        nc.vector.tensor_copy(sc_to[:, 0, 0, :], sc_from[:, 0, 0, :])
        nc.gpsimd.tensor_copy(sc_to[:, 0, 1:PACK, :], sc_from[:, 0, 1:PACK, :])
        nc.gpsimd.tensor_copy(sc_to[:, 1], sc_from[:, 1])

        v_codes, v_sc = [], []
        for h in range(S // BANK):
            part = idx[:, h * BANK // 16 : (h + 1) * BANK // 16]
            codes = keep.tile([P, BANK], U32, name=f"v_codes{h}", align_bytes=64)
            nc.vector.tensor_copy(codes[:], tab_w[:].bitcast(U32).indirect(part))
            sc = keep.tile([P, BANK], U8, name=f"v_sc{h}", align_bytes=64)
            nc.vector.tensor_copy(sc[:], tab_plane[:].indirect(part))
            v_codes.append(codes)
            v_sc.append(sc)

        wb_codes, wb_sc = {}, {}

        def quantise_wb(a, t0, t1):
            slots = t1 - t0
            tag = f"wb_grouped{slots}"
            grouped = keep.tile([P, slots * BANK], BF16, name=tag, tag=tag, align_bytes=64)
            nc.scalar.copy(
                grouped[:].rearrange("p (t m i) -> p m t i", t=slots, i=PACK),
                wb_raw[a][:].rearrange("p i (m t) -> p m t i", t=PACK)[:, :, t0:t1, :],
            )
            codes_tag = f"wb_codes{a}{t0}"
            codes = keep.tile([P, slots * P], U32, name=codes_tag, tag=codes_tag, align_bytes=64)
            sc = keep.tile([P, slots * P], U8, name=f"wb_sc{a}{t0}", align_bytes=64)
            nc.vector.quantize_mx(codes[:].bitcast(FP8X4), sc[:], grouped[:])
            for t in range(t0, t1):
                cols = slice((t - t0) * P, (t - t0 + 1) * P)
                wb_codes[(a, t)] = codes[:, cols]
                wb_sc[(a, t)] = sc[:, cols]

        quantise_wb(0, 0, 1)
        quantise_wb(0, 2, 4)
        quantise_wb(0, 1, 2)

        cab_codes, cab_sc = {}, {}
        half = S2 // 2

        def gather_cab_words(a, h, tag):
            cab_codes[(a, h)] = keep.tile([P, half], U32, name=tag, tag=tag, align_bytes=64)
            part = idx2[:, h * half // 16 : (h + 1) * half // 16]
            nc.vector.tensor_copy(cab_codes[(a, h)][:], tab2_w[a][:].bitcast(U32).indirect(part))

        def gather_cab_scales(h, tag):
            cab_sc[h] = keep.tile([P, half], U8, name=tag, tag=tag, align_bytes=64)
            part = idx2[:, h * half // 16 : (h + 1) * half // 16]
            nc.vector.tensor_copy(cab_sc[h][:], tab2_plane[:].indirect(part))

        def blend_states(engine, t, mix, gate, x, cols, with_factors):
            blend = keep.tile([P, cols.stop - cols.start], F32, name="blend", tag="blend", align_bytes=64)
            engine.tensor_tensor(blend[:], mix[:, cols], gate[:, cols], ALU.mult)
            engine.tensor_tensor(blend[:], x[:, cols], blend[:], ALU.subtract)
            if with_factors:
                engine.tensor_tensor(mix[:, cols], blend[:], factors[t][:, cols], ALU.mult)
            return blend

        def new_states(a, t, units):
            gate = work.tile([P, S], F32, name="gate")
            mix = keep.tile([P, S], F32, name="mix", tag=f"mix{slices.index((a, t)) % 3}", align_bytes=64)
            x = state[(a, t)]
            m0 = t * P
            for h in range(S // BANK):
                cols = slice(h * BANK, (h + 1) * BANK)
                acc_a = psum.tile([P, BANK], F32, name="acc_a", tag="acc_a")
                g0 = a * BANK + m0
                nc.tensor.matmul_mx(
                    acc_a[:], wg_codes[:, 2 * g0 : 2 * (g0 + P)].bitcast(FP4X4), wg_sc[:, g0 : g0 + P],
                    v_codes[h][:].bitcast(FP8X4), v_sc[h][:], start=True, stop=True,
                )
                acc_b = psum.tile([P, BANK], F32, name="acc_b", tag="acc_b")
                nc.tensor.matmul_mx(
                    acc_b[:], wb_codes[(a, t)].bitcast(FP8X4), wb_sc[(a, t)],
                    v_codes[h][:].bitcast(FP8X4), v_sc[h][:], start=True, stop=True,
                )
                nc.scalar.activation(gate[:, cols], acc_a[:], ACT.Sigmoid)
                nc.vector.tensor_tensor(mix[:, cols], x[:, cols], acc_b[:], ALU.subtract)
                if (a, t) == slices[0] and h == 0:
                    blend_states(nc.vector, t, mix, gate, x, cols, True)
            blend = None
            for lo, hi in zip(units, units[1:]):
                if (a, t) != slices[0] or lo > 0:
                    with_factors = (a, t) != slices[-1] or hi < S
                    blend = blend_states(nc.gpsimd, t, mix, gate, x, slice(lo, hi), with_factors)
            return mix, blend

        def scatter(a, t, mix, blend, units):
            for lo, hi in zip(units, units[1:]):
                window = page[(a, t)][:].indirect(idx3[:, lo // 16 : hi // 16])
                if (a, t) == slices[-1] and hi == S:
                    nc.vector.tensor_tensor(window, blend[:], factors[t][:, lo:hi], ALU.mult)
                else:
                    nc.vector.tensor_copy(window, mix[:, lo:hi])

        page_codes, page_sc = {}, {}
        pairs = {}

        def copy_on(engine, dst, src):
            if engine == "scalar":
                nc.scalar.copy(dst, src)
            else:
                nc.vector.tensor_copy(dst, src)

        def round_slice(a, t, engine, cols):
            copy_on(engine, pairs[a][:, t // 2, cols, t % 2], page[(a, t)][:, cols])

        def weave(a, engine, cols, tag):
            woven = keep.tile([P, cols.stop - cols.start, PACK], BF16, name="woven", tag=tag, align_bytes=64)
            copy_on(
                engine,
                woven[:].rearrange("p c (u i) -> p c u i", u=2),
                pairs[a][:, :, cols, :].rearrange("p u c i -> p c u i"),
            )
            return woven

        def quantise_page(a, woven, cols):
            nc.vector.quantize_mx(
                page_codes[a][:, cols].bitcast(FP8X4), page_sc[a][:, cols],
                woven[:].rearrange("p c i -> p (c i)"),
            )

        mixes = {slices[0]: new_states(*slices[0], UNITS[0])}
        quantise_wb(1, 0, PACK)
        for n, (a, t) in enumerate(slices):
            if n + 1 < len(slices):
                mixes[slices[n + 1]] = new_states(*slices[n + 1], UNITS[n + 1])
            scatter(a, t, *mixes[(a, t)], UNITS[n])
            if n == PACK:
                gather_cab_words(0, 0, "cab_codes0")
                gather_cab_words(1, 0, "cab_codes1")
                gather_cab_scales(0, "cab_sc")
            if t == SLOT_ORDER[0]:
                pairs[a] = keep.tile([P, 2, T2, 2], BF16, name="pairs", tag="pairs", align_bytes=64)
            if n + 1 < len(slices):
                round_slice(a, t, "scalar", slice(0, T2))
            if n in (0, 1, 4):
                later = {0: 5, 1: 6, 4: 7}[n]
                page[slices[later]] = load_page(*slices[later])
            if n == PACK - 1:
                halves = [slice(c * T2 // 2, (c + 1) * T2 // 2) for c in range(2)]
                woven_first = [weave(a, "scalar", cols, tag) for cols, tag in zip(halves, ("slot_a", "slot_b"))]

        page_codes[0] = keep.tile([P, T2], U32, name="page_codes0", align_bytes=64)
        page_sc[0] = keep.tile([P, T2], U8, name="page_sc0", tag="blend", align_bytes=64)
        for woven, cols in zip(woven_first, halves):
            quantise_page(0, woven, cols)

        a, t = slices[-1]
        page_codes[a] = keep.tile([P, T2], U32, name="page_codes1", align_bytes=64)
        page_sc[a] = keep.tile([P, T2], U8, name="page_sc1", align_bytes=64)
        chunks = [slice(c * BANK, (c + 1) * BANK) for c in range(T2 // BANK)]
        engines = ("scalar", "scalar", "vector", "vector")
        woven_last = []
        for c in range(T2 // BANK):
            round_slice(a, t, engines[c], chunks[c])
            woven_last.append(weave(a, engines[c], chunks[c], f"state{2 + c}"))
        for c in range(T2 // BANK):
            quantise_page(a, woven_last[c], chunks[c])

        gather_cab_words(0, 1, "state4")
        gather_cab_words(1, 1, "state5")
        gather_cab_scales(1, "state3")

        slot_tags = ("slot_a", "slot_b", "state6", "state7")
        for n in range(S2 // P):
            cabs = slice(n * P, (n + 1) * P)
            own = slice(n % 2 * P, (n % 2 + 1) * P)
            scores = keep.tile([P, T2], F32, name="scores", tag=SCORE_SLOTS[n])
            for c in range(T2 // BANK):
                if n % 2 == 0:
                    acc = psum_e.tile([P, BANK], F32, name="acc_e", tag="acc_e")
                else:
                    tag = "acc_a" if c % 2 == 0 else "acc_b"
                    acc = psum.tile([P, BANK], F32, name=tag, tag=tag)
                for a in range(2):
                    nc.tensor.matmul_mx(
                        acc[:], cab_codes[(a, n // 2)][:, own].bitcast(FP8X4), cab_sc[n // 2][4 * a : P, own],
                        page_codes[a][:, chunks[c]].bitcast(FP8X4), page_sc[a][:, chunks[c]],
                        start=(a == 0), stop=(a == 1),
                    )
                nc.scalar.copy(scores[:, chunks[c]], acc[:])
            picked = keep.tile([P, NPICK], F32, name="picked", tag=slot_tags[n], align_bytes=64)
            last = n == S2 // P - 1
            bounds = (0, 512, 768, 1024) if last else (0, 1024)
            for lo, hi in zip(bounds, bounds[1:]):
                nc.vector.tensor_copy(picked[:, lo:hi], scores[:].indirect(idx4[:, lo // 16 : hi // 16]))
                if last:
                    nc.scalar.activation(picked[:, lo:hi], picked[:, lo:hi], ACT.Identity, bias=bonus_col[:, n : n + 1])
                else:
                    nc.gpsimd.tensor_scalar(
                        picked[:, lo:hi], picked[:, lo:hi], 1.0, bonus_col[:, n : n + 1], ALU.mult, ALU.add
                    )
                nc.sync.dma_start(out[cabs, lo:hi], picked[:, lo:hi])
